import numpy as np
import ml_dtypes


def mxq(x, axis, fmt="e4m3"):
    dtype, down = {"e4m3": (ml_dtypes.float8_e4m3fn, 7), "e5m2": (ml_dtypes.float8_e5m2, 14)}[fmt]
    v = np.moveaxis(np.asarray(x, np.float32).astype(ml_dtypes.bfloat16).astype(np.float64), axis, -1)
    blocks = v.reshape(v.shape[:-1] + (-1, 32))
    amax = np.abs(blocks).max(-1, keepdims=True)
    byte = np.maximum(np.where(amax > 0, np.frexp(amax)[1] - 1 + 127, 0) - down, 1)
    scale = np.exp2(byte - 127.0)
    codes = (blocks / scale).astype(np.float32).astype(dtype).astype(np.float64)
    return np.moveaxis((codes * scale).reshape(v.shape), -1, axis)


WIDE = False


def mx_kscale(k):
    if not WIDE:
        return np.ones(k)
    levels = np.array([10, -10, 5, -5, 0])
    if k % 512:
        return np.exp2(np.random.permutation(np.resize(levels, k // 32))).repeat(32)
    a = np.empty((k // 512, 16))
    for p in range(k // 512):
        a[p, :8] = np.random.permutation(np.resize(levels, 8))
        for g in range(8):
            far = levels[np.abs(levels - a[p, g]) >= 10]
            a[p, g + 8] = far[np.random.randint(len(far))]
    return np.exp2(a.ravel()).repeat(32)


def f64(x):
    return np.asarray(x).astype(np.float64)


def striped(idx):
    return np.tile(idx.reshape(-1, 16).T, (8, 1)).astype(np.uint16)


def unstriped(offs):
    return offs[:16].T.reshape(-1).astype(np.int64)


def pack_weight(w):
    k, n = w.shape
    w = f64(np.asarray(w, np.float32).astype(ml_dtypes.bfloat16)).reshape(k // 32, 32, n)
    amax = np.abs(w).max(1)
    byte = np.clip(np.where(amax > 0, np.frexp(amax)[1] - 1 + 127 - 7, 1), 1, 254)
    scaled = (w * np.exp2(127.0 - byte)[:, None, :]).reshape(k, n).astype(np.float32)
    words = np.ascontiguousarray(scaled.reshape(k // 512, 128, 4, n).transpose(0, 1, 3, 2)).astype(ml_dtypes.float8_e4m3fn).view(np.uint8)
    return words, np.ascontiguousarray(byte.astype(np.uint8).reshape(k // 512, 16, n))


def unpack_weight(words, scales):
    g, p, n, _ = words.shape
    vals = np.ascontiguousarray(words).view(ml_dtypes.float8_e4m3fn).astype(np.float64) * np.repeat(np.exp2(scales.astype(np.float64) - 127.0), 8, axis=1)[..., None]
    return vals.transpose(0, 1, 3, 2).reshape(g * 512, n)


E2M1 = np.array([0.0, 0.5, 1.0, 1.5, 2.0, 3.0, 4.0, 6.0, -0.0, -0.5, -1.0, -1.5, -2.0, -3.0, -4.0, -6.0])


def pack_fp4(w):
    k, n = w.shape
    w = f64(np.asarray(w, np.float32).astype(ml_dtypes.bfloat16)).reshape(k // 32, 32, n)
    amax = np.abs(w).max(1)
    mant, ex = np.frexp(amax / 6.0)
    byte = np.clip(np.where(amax > 0, np.where(mant > 0.5, ex, ex - 1) + 127, 1), 1, 254)
    scaled = (w * np.exp2(127.0 - byte)[:, None, :]).reshape(k, n).astype(np.float32)
    c = np.ascontiguousarray(scaled.reshape(k // 512, 128, 4, n).transpose(0, 1, 3, 2)).astype(ml_dtypes.float4_e2m1fn).view(np.uint8) & 0xF
    words = (c[..., 0::2] | (c[..., 1::2] << 4)).reshape(k // 512, 128, 2 * n)
    return np.ascontiguousarray(words), np.ascontiguousarray(byte.astype(np.uint8).reshape(k // 512, 16, n))


def unpack_fp4(words, scales):
    g, _, n = scales.shape
    words = np.ascontiguousarray(words).reshape(g, 128, n, 2)
    nib = np.empty((g, 128, n, 4), np.uint8)
    nib[..., 0::2] = words & 0xF
    nib[..., 1::2] = words >> 4
    vals = E2M1[nib] * np.repeat(np.exp2(scales.astype(np.float64) - 127.0), 8, axis=1)[..., None]
    return vals.transpose(0, 1, 3, 2).reshape(g * 512, n)


def planes(y):
    n, m = y.shape
    v = y.astype(np.float32).astype(ml_dtypes.bfloat16).astype(np.float64).reshape(n // 32, 32, m)
    top = np.abs(v).max(1)
    byte = np.clip(np.where(top > 0, np.frexp(top)[1] - 1 + 127 - 7, 1), 1, 254)
    codes = (v * np.exp2(127.0 - byte)[:, None, :]).reshape(n, m).astype(np.float32).astype(ml_dtypes.float8_e4m3fn).view(np.uint8)
    words = codes.reshape(n // 512, 128, 4, m).transpose(0, 1, 3, 2)
    return np.ascontiguousarray(words), np.ascontiguousarray(byte.astype(np.uint8).reshape(n // 512, 16, m))


def relu(v):
    return np.maximum(v, 0.0)


K, T, S, J, H, N, W = 1536, 2048, 512, 512, 512, 512, 2048


def setup_inputs():
    n = np.random.standard_normal
    s = mx_kscale(K)[:, None]
    u = mx_kscale(H)
    r = mx_kscale(J)[:, None]
    packed_xT = pack_weight(n((K, T)) * s)
    packed_eT = pack_weight(n((J, W)) * r)
    packed_w3 = pack_fp4(n((H, N)) / np.sqrt(H) / u[:, None])
    return {
        "x_words": packed_xT[0],
        "x_scales": packed_xT[1],
        "e_words": packed_eT[0],
        "e_scales": packed_eT[1],
        "w1": (n((K, H)) / np.sqrt(2 * K) / s * u).astype(np.float32),
        "w2": (n((J, H)) / np.sqrt(2 * J) / r * u).astype(np.float32),
        "w3_words": packed_w3[0],
        "w3_scales": packed_w3[1],
        "bias": (0.3 * n((H, 1)) * u[:, None]).astype(np.float32),
        "offs": striped(np.random.permutation(T)[:S]),
        "item": striped(np.random.permutation(W)[:S]),
    }


def reference(x_words, x_scales, e_words, e_scales, w1, w2, w3_words, w3_scales, bias, offs, item):
    xq = unpack_weight(x_words, x_scales)[:, unstriped(offs)]
    e_item = unpack_weight(e_words, e_scales)[:, unstriped(item)]
    h = relu((mxq(f64(w1), 0, "e4m3").T @ xq + mxq(f64(w2), 0, "e4m3").T @ e_item) + f64(bias))
    out_0 = unpack_fp4(w3_words, w3_scales).T @ mxq(h, 0, "e4m3")
    return (out_0,) + planes(out_0)

@@ -1,0 +1,211 @@
+from contextlib import ExitStack
+
+import concourse.mybir as mybir
+
+F32 = mybir.dt.float32
+BF16 = mybir.dt.bfloat16
+I32 = mybir.dt.int32
+U32 = mybir.dt.uint32
+U16 = mybir.dt.uint16
+U8 = mybir.dt.uint8
+FP8X4 = mybir.dt.float8_e4m3fn_x4
+FP4X4 = mybir.dt.float4_e2m1fn_x4
+ACT = mybir.ActivationFunctionType
+ALU = mybir.AluOpType
+
+P = 128
+PACK = 4
+K_PASS = P * PACK
+TABLE = 2048
+PAIRS = 512
+WIDTH = 512
+HALF = 256
+CHUNK = 128
+QUADS = 4
+RUN = 4
+
+FLOPS = 2 * PAIRS * WIDTH * (1536 + 512 + 512)
+
+
+def tile_picked_zuit_relu_po_kernel(
+    tc, x_words, x_scales, e_words, e_scales, w1, w2, w3_words, w3_scales, bias, offs, item, out_0, out_1, out_2
+):
+    nc = tc.nc
+    x_passes = x_words.shape[0]
+    passes = x_passes + 1
+
+    with ExitStack() as ctx:
+        keep = ctx.enter_context(tc.tile_pool(name="keep", bufs=1))
+        psum = ctx.enter_context(tc.psum_pool(name="psum", bufs=1))
+
+        def sbuf(name, shape, dtype):
+            return keep.tile(shape, dtype, name=name, align_bytes=64)
+
+        offs_sb = keep.tile([P, PAIRS // 16], U16, name="offs_sb")
+        item_sb = keep.tile([P, PAIRS // 16], U16, name="item_sb")
+        bias_sb = sbuf("bias_sb", [P, PACK], F32)
+        w3_raw = sbuf("w3_raw", [P, 2 * WIDTH], U8)
+        w3s_raw = sbuf("w3s_raw", [P, WIDTH], U8)
+        xs_table = sbuf("xs_table", [P, TABLE], U8)
+        es_table = sbuf("es_table", [P, TABLE], U8)
+        w_raw = [sbuf(f"w_raw{g}", [P, PACK, WIDTH], F32) for g in range(passes)]
+        word_table = [sbuf(f"word_table{g}", [P, TABLE], I32) for g in range(passes)]
+
+        w_rows = [w1[K_PASS * g : K_PASS * (g + 1), :] for g in range(x_passes)] + [w2]
+        word_rows = [x_words[g] for g in range(x_passes)] + [e_words[0]]
+        lists = [offs_sb] * x_passes + [item_sb]
+        pass_order = [0, 1, 3, 2]
+
+        nc.gpsimd.memset(xs_table[:].bitcast(I32), 0)
+        nc.vector.memset(es_table[:].bitcast(I32), 0)
+        nc.vector.memset(w3s_raw[:].bitcast(I32), 0)
+        e_row = PACK * x_passes
+
+        def load_weights(g):
+            nc.sync.dma_start(out=w_raw[g][:], in_=w_rows[g].rearrange("(p j) c -> p j c", j=PACK))
+
+        for q in range(QUADS):
+            nc.gpsimd.dma_start(
+                out=xs_table[32 * q : 32 * q + PACK * x_passes, :].bitcast(I32),
+                in_=x_scales[:, 4 * q : 4 * q + 4, :].bitcast(I32),
+            )
+
+        load_weights(pass_order[0])
+        nc.sync.dma_start(out=bias_sb[:], in_=bias.rearrange("(p t) o -> p (t o)", t=PACK))
+        nc.sync.dma_start(out=w3_raw[:].bitcast(I32), in_=w3_words[0].bitcast(I32))
+        load_weights(pass_order[1])
+        for q in range(QUADS):
+            nc.sync.dma_start(
+                out=es_table[32 * q + e_row : 32 * q + e_row + 4, :].bitcast(I32),
+                in_=e_scales[0, 4 * q : 4 * q + 4, :].bitcast(I32),
+            )
+        load_weights(pass_order[2])
+        nc.sync.dma_start(offs_sb[:], offs)
+        nc.sync.dma_start(item_sb[:], item)
+        load_weights(pass_order[3])
+        for q in range(QUADS):
+            nc.sync.dma_start(
+                out=w3s_raw[32 * q : 32 * q + 4, :].bitcast(I32),
+                in_=w3_scales[0, 4 * q : 4 * q + 4, :].bitcast(I32),
+            )
+        for g in pass_order:
+            nc.sync.dma_start(out=word_table[g][:], in_=word_rows[g].rearrange("p n t -> p (n t)").bitcast(I32))
+
+        w_codes, w_scales = {}, {}
+        for g in pass_order:
+            grouped = sbuf(f"w_grouped{g}", [P, PACK * WIDTH], BF16)
+            nc.scalar.activation(
+                out=grouped[:].rearrange("p (t m j) -> p m j t", t=PACK, j=PACK),
+                in_=w_raw[g][:].rearrange("p j (m t) -> p m j t", t=PACK),
+                func=ACT.Copy,
+            )
+            w_codes[g] = sbuf(f"w_codes{g}", [P, WIDTH], U32)
+            w_scales[g] = sbuf(f"w_scales{g}", [P, WIDTH], U8)
+            nc.vector.quantize_mx(out=w_codes[g][:].bitcast(FP8X4), scales=w_scales[g][:], in_=grouped[:])
+
+        xs_picked = sbuf("xs_picked", [P, PAIRS], U8)
+        es_picked = sbuf("es_picked", [P, PAIRS], U8)
+        nc.vector.tensor_copy(xs_picked[:], xs_table[:].indirect(offs_sb[:]))
+        nc.vector.tensor_copy(es_picked[:], es_table[:].indirect(item_sb[:]))
+        picked_scales = [xs_picked] * x_passes + [es_picked]
+
+        w3_codes = sbuf("w3_codes", [P, 2 * WIDTH], U8)
+        w3_plane = sbuf("w3_plane", [P, WIDTH], U8)
+        nc.vector.tensor_copy(
+            out=w3_codes[:].rearrange("p (t m b) -> p m t b", t=PACK, b=2),
+            in_=w3_raw[:].rearrange("p (m t b) -> p m t b", t=PACK, b=2),
+        )
+        nc.vector.tensor_copy(
+            out=w3_plane[:].rearrange("p (t m) -> p m t", t=PACK),
+            in_=w3s_raw[:].rearrange("p (m t) -> p m t", t=PACK),
+        )
+
+        halves = PAIRS // HALF
+        banks = [[psum.tile([P, 512], F32, name=f"bank{h}_{t}") for t in range(PACK)] for h in range(halves)]
+
+        for n, g in enumerate(pass_order):
+            for h in range(halves):
+                picked = sbuf(f"picked{g}_{h}", [P, HALF], U32)
+                entries = lists[g][:, h * HALF // 16 : (h + 1) * HALF // 16]
+                nc.vector.tensor_copy(picked[:], word_table[g][:].bitcast(U32).indirect(entries))
+                for t in range(PACK):
+                    cols = slice(P * t, P * (t + 1))
+                    nc.tensor.matmul_mx(
+                        out=banks[h][t][:, :HALF],
+                        lhsT=w_codes[g][:, cols].bitcast(FP8X4),
+                        lhsT_scale=w_scales[g][:, cols],
+                        rhs=picked[:].bitcast(FP8X4),
+                        rhs_scale=picked_scales[g][PACK * g :, h * HALF : (h + 1) * HALF],
+                        start=(n == 0),
+                        stop=(n == passes - 1),
+                    )
+
+        def interleave(name, rows):
+            woven = sbuf(name, [P, PACK * CHUNK], BF16)
+            nc.vector.tensor_copy(
+                out=woven[:].rearrange("p (c i t) -> p c t i", i=RUN, t=PACK),
+                in_=rows.rearrange("p t (c i) -> p c t i", i=RUN),
+            )
+            return woven
+
+        y_codes = sbuf("y_codes", [P, PAIRS], U32)
+        y_plane = sbuf("y_plane", [P, PAIRS], U8)
+        out_rows = out_0.rearrange("(p t) j -> p t j", t=PACK)
+        out_words = out_1[0].rearrange("p n t -> p (n t)").bitcast(I32)
+
+        def relu(hid, h, t, cols, on_vector):
+            src = banks[h][t][:, cols]
+            if on_vector:
+                nc.vector.tensor_scalar(
+                    out=hid[:, t, :], in0=src, scalar1=bias_sb[:, t : t + 1], scalar2=0.0, op0=ALU.add, op1=ALU.max
+                )
+            else:
+                nc.scalar.activation(out=hid[:, t, :], in_=src, func=ACT.Relu, bias=bias_sb[:, t : t + 1])
+
+        per_half = HALF // CHUNK
+        chunks = PAIRS // CHUNK
+        results = []
+
+        def second_layer(c, woven):
+            h_codes = sbuf(f"h_codes{c}", [P, CHUNK], U32)
+            h_plane = sbuf(f"h_plane{c}", [P, CHUNK], U8)
+            nc.vector.quantize_mx(out=h_codes[:].bitcast(FP8X4), scales=h_plane[:], in_=woven[:])
+            bank = banks[0][c]
+            for t in range(PACK):
+                nc.tensor.matmul_mx(
+                    out=bank[:, CHUNK * t : CHUNK * (t + 1)],
+                    lhsT=w3_codes[:, 2 * P * t : 2 * P * (t + 1)].bitcast(FP4X4),
+                    lhsT_scale=w3_plane[:, P * t : P * (t + 1)],
+                    rhs=h_codes[:].bitcast(FP8X4),
+                    rhs_scale=h_plane[:],
+                    start=True,
+                    stop=True,
+                )
+            results.append(bank)
+
+        hidden = []
+        for c in range(chunks):
+            hid = sbuf(f"hidden{c}", [P, PACK, CHUNK], BF16)
+            hidden.append(hid)
+            h, lo = c // per_half, CHUNK * (c % per_half)
+            for t in range(PACK):
+                relu(hid, h, t, slice(lo, lo + CHUNK), t >= 2 + c)
+        for c in range(chunks):
+            second_layer(c, interleave(f"h_woven{c}", hidden[c][:]))
+
+        for c in range(chunks):
+            cols = slice(CHUNK * c, CHUNK * (c + 1))
+            y = sbuf(f"y{c}", [P, PACK, CHUNK], F32)
+            nc.scalar.activation(out=y[:].rearrange("p t j -> p (t j)"), in_=results[c][:], func=ACT.Copy)
+            nc.sync.dma_start(out=out_rows[:, :, cols], in_=y[:])
+            woven = interleave(f"y_woven{c}", y[:])
+            nc.vector.quantize_mx(out=y_codes[:, cols].bitcast(FP8X4), scales=y_plane[:, cols], in_=woven[:])
+            if c % per_half == per_half - 1:
+                half_cols = slice(CHUNK * (c + 1) - HALF, CHUNK * (c + 1))
+                nc.sync.dma_start(out=out_words[:, half_cols], in_=y_codes[:, half_cols].bitcast(I32))
+
+        for q in range(QUADS):
+            queue = nc.scalar if q % 2 else nc.sync
+            queue.dma_start(
+                out=out_2[0, 4 * q : 4 * q + 4, :].bitcast(I32), in_=y_plane[32 * q : 32 * q + 4, :].bitcast(I32)
+            )

@@ -140,7 +140,7 @@ def tile_picked_zuit_relu_po_kernel(
                         stop=(n == passes - 1),
                     )
 
-        def interleave(name, rows):
+        def weave(name, rows):
             woven = sbuf(name, [P, PACK * CHUNK], BF16)
             nc.vector.tensor_copy(
                 out=woven[:].rearrange("p (c i t) -> p c t i", i=RUN, t=PACK),
@@ -148,61 +148,59 @@ def tile_picked_zuit_relu_po_kernel(
             )
             return woven
 
+        def quantise_half(name, rows, codes, plane):
+            spans = [slice(lo, lo + CHUNK) for lo in range(0, HALF, CHUNK)]
+            woven = [weave(f"{name}{n}", rows[:, :, span]) for n, span in enumerate(spans)]
+            for span, tile in zip(spans, woven):
+                nc.vector.quantize_mx(out=codes[:, span].bitcast(FP8X4), scales=plane[:, span], in_=tile[:])
+
         y_codes = sbuf("y_codes", [P, PAIRS], U32)
         y_plane = sbuf("y_plane", [P, PAIRS], U8)
         out_rows = out_0.rearrange("(p t) j -> p t j", t=PACK)
         out_words = out_1[0].rearrange("p n t -> p (n t)").bitcast(I32)
 
-        def relu(hid, h, t, cols, on_vector):
-            src = banks[h][t][:, cols]
-            if on_vector:
-                nc.vector.tensor_scalar(
-                    out=hid[:, t, :], in0=src, scalar1=bias_sb[:, t : t + 1], scalar2=0.0, op0=ALU.add, op1=ALU.max
-                )
-            else:
-                nc.scalar.activation(out=hid[:, t, :], in_=src, func=ACT.Relu, bias=bias_sb[:, t : t + 1])
-
-        per_half = HALF // CHUNK
-        chunks = PAIRS // CHUNK
-        results = []
-
-        def second_layer(c, woven):
-            h_codes = sbuf(f"h_codes{c}", [P, CHUNK], U32)
-            h_plane = sbuf(f"h_plane{c}", [P, CHUNK], U8)
-            nc.vector.quantize_mx(out=h_codes[:].bitcast(FP8X4), scales=h_plane[:], in_=woven[:])
-            bank = banks[0][c]
-            for t in range(PACK):
-                nc.tensor.matmul_mx(
-                    out=bank[:, CHUNK * t : CHUNK * (t + 1)],
-                    lhsT=w3_codes[:, 2 * P * t : 2 * P * (t + 1)].bitcast(FP4X4),
-                    lhsT_scale=w3_plane[:, P * t : P * (t + 1)],
-                    rhs=h_codes[:].bitcast(FP8X4),
-                    rhs_scale=h_plane[:],
-                    start=True,
-                    stop=True,
-                )
-            results.append(bank)
-
         hidden = []
-        for c in range(chunks):
-            hid = sbuf(f"hidden{c}", [P, PACK, CHUNK], BF16)
+        for h in range(halves):
+            hid = sbuf(f"hidden{h}", [P, PACK, HALF], BF16)
             hidden.append(hid)
-            h, lo = c // per_half, CHUNK * (c % per_half)
             for t in range(PACK):
-                relu(hid, h, t, slice(lo, lo + CHUNK), t >= 2 + c)
-        for c in range(chunks):
-            second_layer(c, interleave(f"h_woven{c}", hidden[c][:]))
+                src = banks[h][t][:, :HALF]
+                if h == 0 and t >= 2:
+                    nc.vector.tensor_scalar(
+                        out=hid[:, t, :], in0=src, scalar1=bias_sb[:, t : t + 1], scalar2=0.0, op0=ALU.add, op1=ALU.max
+                    )
+                else:
+                    nc.scalar.activation(out=hid[:, t, :], in_=src, func=ACT.Relu, bias=bias_sb[:, t : t + 1])
 
-        for c in range(chunks):
-            cols = slice(CHUNK * c, CHUNK * (c + 1))
-            y = sbuf(f"y{c}", [P, PACK, CHUNK], F32)
-            nc.scalar.activation(out=y[:].rearrange("p t j -> p (t j)"), in_=results[c][:], func=ACT.Copy)
-            nc.sync.dma_start(out=out_rows[:, :, cols], in_=y[:])
-            woven = interleave(f"y_woven{c}", y[:])
-            nc.vector.quantize_mx(out=y_codes[:, cols].bitcast(FP8X4), scales=y_plane[:, cols], in_=woven[:])
-            if c % per_half == per_half - 1:
-                half_cols = slice(CHUNK * (c + 1) - HALF, CHUNK * (c + 1))
-                nc.sync.dma_start(out=out_words[:, half_cols], in_=y_codes[:, half_cols].bitcast(I32))
+        ys = []
+        for h in range(halves):
+            cols = slice(HALF * h, HALF * (h + 1))
+            h_codes = sbuf(f"h_codes{h}", [P, HALF], U32)
+            h_plane = sbuf(f"h_plane{h}", [P, HALF], U8)
+            quantise_half(f"h_woven{h}_", hidden[h][:], h_codes[:], h_plane[:])
+            y = sbuf(f"y{h}", [P, PACK, HALF], F32)
+            ys.append(y)
+            for u in range(2):
+                bank = banks[0][2 * h + u]
+                for e in range(2):
+                    t = 2 * u + e
+                    nc.tensor.matmul_mx(
+                        out=bank[:, HALF * e : HALF * (e + 1)],
+                        lhsT=w3_codes[:, 2 * P * t : 2 * P * (t + 1)].bitcast(FP4X4),
+                        lhsT_scale=w3_plane[:, P * t : P * (t + 1)],
+                        rhs=h_codes[:].bitcast(FP8X4),
+                        rhs_scale=h_plane[:],
+                        start=True,
+                        stop=True,
+                    )
+                rows = y[:, 2 * u : 2 * u + 2, :]
+                nc.scalar.activation(out=rows.rearrange("p t j -> p (t j)"), in_=bank[:], func=ACT.Copy)
+                nc.sync.dma_start(out=out_rows[:, 2 * u : 2 * u + 2, cols], in_=rows)
+
+        for h in range(halves):
+            cols = slice(HALF * h, HALF * (h + 1))
+            quantise_half(f"y_woven{h}_", ys[h][:], y_codes[:, cols], y_plane[:, cols])
+            nc.sync.dma_start(out=out_words[:, cols], in_=y_codes[:, cols].bitcast(I32))
 
         for q in range(QUADS):
             queue = nc.scalar if q % 2 else nc.sync

@@ -148,44 +148,44 @@ def tile_picked_zuit_relu_po_kernel(
             )
             return woven
 
-        def quantise_half(name, rows, codes, plane):
-            spans = [slice(lo, lo + CHUNK) for lo in range(0, HALF, CHUNK)]
-            woven = [weave(f"{name}{n}", rows[:, :, span]) for n, span in enumerate(spans)]
-            for span, tile in zip(spans, woven):
-                nc.vector.quantize_mx(out=codes[:, span].bitcast(FP8X4), scales=plane[:, span], in_=tile[:])
-
         y_codes = sbuf("y_codes", [P, PAIRS], U32)
         y_plane = sbuf("y_plane", [P, PAIRS], U8)
         out_rows = out_0.rearrange("(p t) j -> p t j", t=PACK)
         out_words = out_1[0].rearrange("p n t -> p (n t)").bitcast(I32)
+        spans = [slice(lo, lo + CHUNK) for lo in range(0, HALF, CHUNK)]
+        row_pairs = [slice(0, 2), slice(2, 4)]
 
-        hidden = []
-        for h in range(halves):
-            hid = sbuf(f"hidden{h}", [P, PACK, HALF], BF16)
-            hidden.append(hid)
+        hidden = [sbuf(f"hidden{h}", [P, PACK, HALF], BF16) for h in range(halves)]
+        for span in spans:
             for t in range(PACK):
-                src = banks[h][t][:, :HALF]
-                if h == 0 and t >= 2:
+                src = banks[0][t][:, span]
+                if t % 2:
                     nc.vector.tensor_scalar(
-                        out=hid[:, t, :], in0=src, scalar1=bias_sb[:, t : t + 1], scalar2=0.0, op0=ALU.add, op1=ALU.max
+                        out=hidden[0][:, t, span],
+                        in0=src,
+                        scalar1=bias_sb[:, t : t + 1],
+                        scalar2=0.0,
+                        op0=ALU.add,
+                        op1=ALU.max,
                     )
                 else:
-                    nc.scalar.activation(out=hid[:, t, :], in_=src, func=ACT.Relu, bias=bias_sb[:, t : t + 1])
+                    nc.scalar.activation(out=hidden[0][:, t, span], in_=src, func=ACT.Relu, bias=bias_sb[:, t : t + 1])
+        for t in range(PACK):
+            nc.scalar.activation(
+                out=hidden[1][:, t, :], in_=banks[1][t][:, :HALF], func=ACT.Relu, bias=bias_sb[:, t : t + 1]
+            )
 
-        ys = []
+        results = []
         for h in range(halves):
-            cols = slice(HALF * h, HALF * (h + 1))
-            h_codes = sbuf(f"h_codes{h}", [P, HALF], U32)
-            h_plane = sbuf(f"h_plane{h}", [P, HALF], U8)
-            quantise_half(f"h_woven{h}_", hidden[h][:], h_codes[:], h_plane[:])
-            y = sbuf(f"y{h}", [P, PACK, HALF], F32)
-            ys.append(y)
-            for u in range(2):
-                bank = banks[0][2 * h + u]
-                for e in range(2):
-                    t = 2 * u + e
+            woven = [weave(f"h_woven{h}_{n}", hidden[h][:, :, span]) for n, span in enumerate(spans)]
+            for n, tile in enumerate(woven):
+                h_codes = sbuf(f"h_codes{h}_{n}", [P, CHUNK], U32)
+                h_plane = sbuf(f"h_plane{h}_{n}", [P, CHUNK], U8)
+                nc.vector.quantize_mx(out=h_codes[:].bitcast(FP8X4), scales=h_plane[:], in_=tile[:])
+                bank = banks[0][len(results)]
+                for t in range(PACK):
                     nc.tensor.matmul_mx(
-                        out=bank[:, HALF * e : HALF * (e + 1)],
+                        out=bank[:, CHUNK * t : CHUNK * (t + 1)],
                         lhsT=w3_codes[:, 2 * P * t : 2 * P * (t + 1)].bitcast(FP4X4),
                         lhsT_scale=w3_plane[:, P * t : P * (t + 1)],
                         rhs=h_codes[:].bitcast(FP8X4),
@@ -193,13 +193,24 @@ def tile_picked_zuit_relu_po_kernel(
                         start=True,
                         stop=True,
                     )
-                rows = y[:, 2 * u : 2 * u + 2, :]
-                nc.scalar.activation(out=rows.rearrange("p t j -> p (t j)"), in_=bank[:], func=ACT.Copy)
-                nc.sync.dma_start(out=out_rows[:, 2 * u : 2 * u + 2, cols], in_=rows)
+                results.append(bank[:].rearrange("p (t j) -> p t j", t=PACK))
+
+        ys = []
+        for h in range(halves):
+            cols = slice(HALF * h, HALF * (h + 1))
+            y = sbuf(f"y{h}", [P, PACK, HALF], F32)
+            ys.append(y)
+            nc.scalar.activation(out=y[:, :, spans[0]], in_=results[2 * h], func=ACT.Copy)
+            for rows in row_pairs:
+                nc.scalar.activation(out=y[:, rows, spans[1]], in_=results[2 * h + 1][:, rows, :], func=ACT.Copy)
+                nc.sync.dma_start(out=out_rows[:, rows, cols], in_=y[:, rows, :])
 
         for h in range(halves):
             cols = slice(HALF * h, HALF * (h + 1))
-            quantise_half(f"y_woven{h}_", ys[h][:], y_codes[:, cols], y_plane[:, cols])
+            woven = [weave(f"y_woven{h}_{n}", ys[h][:, :, span]) for n, span in enumerate(spans)]
+            for n, tile in enumerate(woven):
+                piece = slice(HALF * h + CHUNK * n, HALF * h + CHUNK * (n + 1))
+                nc.vector.quantize_mx(out=y_codes[:, piece].bitcast(FP8X4), scales=y_plane[:, piece], in_=tile[:])
             nc.sync.dma_start(out=out_words[:, cols], in_=y_codes[:, cols].bitcast(I32))
 
         for q in range(QUADS):

@@ -38,8 +38,8 @@ def tile_picked_zuit_relu_po_kernel(
         keep = ctx.enter_context(tc.tile_pool(name="keep", bufs=1))
         psum = ctx.enter_context(tc.psum_pool(name="psum", bufs=1))
 
-        def sbuf(name, shape, dtype):
-            return keep.tile(shape, dtype, name=name, align_bytes=64)
+        def sbuf(name, shape, dtype, tag=None):
+            return keep.tile(shape, dtype, name=name, tag=tag or name, align_bytes=64)
 
         offs_sb = keep.tile([P, PAIRS // 16], U16, name="offs_sb")
         item_sb = keep.tile([P, PAIRS // 16], U16, name="item_sb")
@@ -140,8 +140,8 @@ def tile_picked_zuit_relu_po_kernel(
                         stop=(n == passes - 1),
                     )
 
-        def weave(name, rows):
-            woven = sbuf(name, [P, PACK * CHUNK], BF16)
+        def weave(name, rows, tag=None):
+            woven = sbuf(name, [P, PACK * CHUNK], BF16, tag=tag)
             nc.vector.tensor_copy(
                 out=woven[:].rearrange("p (c i t) -> p c t i", i=RUN, t=PACK),
                 in_=rows.rearrange("p t (c i) -> p c t i", i=RUN),
@@ -156,62 +156,65 @@ def tile_picked_zuit_relu_po_kernel(
         row_pairs = [slice(0, 2), slice(2, 4)]
 
         hidden = [sbuf(f"hidden{h}", [P, PACK, HALF], BF16) for h in range(halves)]
-        for span in spans:
-            for t in range(PACK):
-                src = banks[0][t][:, span]
-                if t % 2:
-                    nc.vector.tensor_scalar(
-                        out=hidden[0][:, t, span],
-                        in0=src,
-                        scalar1=bias_sb[:, t : t + 1],
-                        scalar2=0.0,
-                        op0=ALU.add,
-                        op1=ALU.max,
-                    )
-                else:
-                    nc.scalar.activation(out=hidden[0][:, t, span], in_=src, func=ACT.Relu, bias=bias_sb[:, t : t + 1])
         for t in range(PACK):
+            if t % 2 == 0:
+                nc.scalar.activation(
+                    out=hidden[0][:, t, :], in_=banks[0][t][:, :HALF], func=ACT.Relu, bias=bias_sb[:, t : t + 1]
+                )
+                continue
+            for span in spans if t == PACK - 1 else [slice(0, HALF)]:
+                nc.vector.tensor_scalar(
+                    out=hidden[0][:, t, span],
+                    in0=banks[0][t][:, span],
+                    scalar1=bias_sb[:, t : t + 1],
+                    scalar2=0.0,
+                    op0=ALU.add,
+                    op1=ALU.max,
+                )
+        pieces = [(t, slice(0, HALF)) for t in range(2)] + [(t, span) for span in spans for t in range(2, PACK)]
+        for t, span in pieces:
             nc.scalar.activation(
-                out=hidden[1][:, t, :], in_=banks[1][t][:, :HALF], func=ACT.Relu, bias=bias_sb[:, t : t + 1]
+                out=hidden[1][:, t, span], in_=banks[1][t][:, span], func=ACT.Relu, bias=bias_sb[:, t : t + 1]
             )
 
-        results = []
+        h_codes, h_plane = [], []
         for h in range(halves):
             woven = [weave(f"h_woven{h}_{n}", hidden[h][:, :, span]) for n, span in enumerate(spans)]
-            for n, tile in enumerate(woven):
-                h_codes = sbuf(f"h_codes{h}_{n}", [P, CHUNK], U32)
-                h_plane = sbuf(f"h_plane{h}_{n}", [P, CHUNK], U8)
-                nc.vector.quantize_mx(out=h_codes[:].bitcast(FP8X4), scales=h_plane[:], in_=tile[:])
-                bank = banks[0][len(results)]
-                for t in range(PACK):
-                    nc.tensor.matmul_mx(
-                        out=bank[:, CHUNK * t : CHUNK * (t + 1)],
-                        lhsT=w3_codes[:, 2 * P * t : 2 * P * (t + 1)].bitcast(FP4X4),
-                        lhsT_scale=w3_plane[:, P * t : P * (t + 1)],
-                        rhs=h_codes[:].bitcast(FP8X4),
-                        rhs_scale=h_plane[:],
-                        start=True,
-                        stop=True,
-                    )
-                results.append(bank[:].rearrange("p (t j) -> p t j", t=PACK))
+            h_codes.append(sbuf(f"h_codes{h}", [P, HALF], U32))
+            h_plane.append(sbuf(f"h_plane{h}", [P, HALF], U8))
+            for span, tile in zip(spans, woven):
+                nc.vector.quantize_mx(out=h_codes[h][:, span].bitcast(FP8X4), scales=h_plane[h][:, span], in_=tile[:])
 
+        result_banks = [banks[0][0], banks[0][1], banks[1][3], banks[0][2], banks[0][3]] + banks[1][:3]
         ys = []
         for h in range(halves):
             cols = slice(HALF * h, HALF * (h + 1))
             y = sbuf(f"y{h}", [P, PACK, HALF], F32)
             ys.append(y)
-            nc.scalar.activation(out=y[:, :, spans[0]], in_=results[2 * h], func=ACT.Copy)
-            for rows in row_pairs:
-                nc.scalar.activation(out=y[:, rows, spans[1]], in_=results[2 * h + 1][:, rows, :], func=ACT.Copy)
+            for u, rows in enumerate(row_pairs):
+                for n, span in enumerate(spans):
+                    bank = result_banks[4 * h + 2 * u + n]
+                    for e in range(2):
+                        t = 2 * u + e
+                        nc.tensor.matmul_mx(
+                            out=bank[:, CHUNK * e : CHUNK * (e + 1)],
+                            lhsT=w3_codes[:, 2 * P * t : 2 * P * (t + 1)].bitcast(FP4X4),
+                            lhsT_scale=w3_plane[:, P * t : P * (t + 1)],
+                            rhs=h_codes[h][:, span].bitcast(FP8X4),
+                            rhs_scale=h_plane[h][:, span],
+                            start=True,
+                            stop=True,
+                        )
+                    pair = bank[:, : 2 * CHUNK].rearrange("p (e j) -> p e j", e=2)
+                    nc.scalar.activation(out=y[:, rows, span], in_=pair, func=ACT.Copy)
                 nc.sync.dma_start(out=out_rows[:, rows, cols], in_=y[:, rows, :])
 
         for h in range(halves):
-            cols = slice(HALF * h, HALF * (h + 1))
-            woven = [weave(f"y_woven{h}_{n}", ys[h][:, :, span]) for n, span in enumerate(spans)]
+            woven = [weave(f"y_woven{h}_{n}", ys[h][:, :, span], f"h_woven{1 - h}_{1 - n}") for n, span in enumerate(spans)]
             for n, tile in enumerate(woven):
                 piece = slice(HALF * h + CHUNK * n, HALF * h + CHUNK * (n + 1))
                 nc.vector.quantize_mx(out=y_codes[:, piece].bitcast(FP8X4), scales=y_plane[:, piece], in_=tile[:])
-            nc.sync.dma_start(out=out_words[:, cols], in_=y_codes[:, cols].bitcast(I32))
+        nc.sync.dma_start(out=out_words, in_=y_codes[:].bitcast(I32))
 
         for q in range(QUADS):
             queue = nc.scalar if q % 2 else nc.sync

@@ -186,11 +186,11 @@ def tile_picked_zuit_relu_po_kernel(
                 nc.vector.quantize_mx(out=h_codes[h][:, span].bitcast(FP8X4), scales=h_plane[h][:, span], in_=tile[:])
 
         result_banks = [banks[0][0], banks[0][1], banks[1][3], banks[0][2], banks[0][3]] + banks[1][:3]
-        ys = []
+        y = sbuf("y", [P, PACK, PAIRS], F32)
+        y_flat = y[:].rearrange("p t j -> p (t j)")
+        out_flat = out_0.rearrange("(p t) j -> p (t j)", t=PACK)
         for h in range(halves):
             cols = slice(HALF * h, HALF * (h + 1))
-            y = sbuf(f"y{h}", [P, PACK, HALF], F32)
-            ys.append(y)
             for u, rows in enumerate(row_pairs):
                 for n, span in enumerate(spans):
                     bank = result_banks[4 * h + 2 * u + n]
@@ -206,15 +206,23 @@ def tile_picked_zuit_relu_po_kernel(
                             stop=True,
                         )
                     pair = bank[:, : 2 * CHUNK].rearrange("p (e j) -> p e j", e=2)
-                    nc.scalar.activation(out=y[:, rows, span], in_=pair, func=ACT.Copy)
-                nc.sync.dma_start(out=out_rows[:, rows, cols], in_=y[:, rows, :])
+                    piece = slice(HALF * h + span.start, HALF * h + span.stop)
+                    nc.scalar.activation(out=y[:, rows, piece], in_=pair, func=ACT.Copy)
+                if u == 0:
+                    nc.sync.dma_start(out=out_rows[:, rows, cols], in_=y[:, rows, cols])
+                elif h == 0:
+                    nc.sync.dma_start(out=out_rows[:, 2, cols], in_=y[:, 2, cols])
+                else:
+                    tail = slice(2 * PAIRS + HALF, PACK * PAIRS)
+                    nc.sync.dma_start(out=out_flat[:, tail], in_=y_flat[:, tail])
 
         for h in range(halves):
-            woven = [weave(f"y_woven{h}_{n}", ys[h][:, :, span], f"h_woven{1 - h}_{1 - n}") for n, span in enumerate(spans)]
+            cols = slice(HALF * h, HALF * (h + 1))
+            woven = [weave(f"y_woven{h}_{n}", y[:, :, HALF * h + span.start : HALF * h + span.stop], f"h_woven{1 - h}_{1 - n}") for n, span in enumerate(spans)]
             for n, tile in enumerate(woven):
                 piece = slice(HALF * h + CHUNK * n, HALF * h + CHUNK * (n + 1))
                 nc.vector.quantize_mx(out=y_codes[:, piece].bitcast(FP8X4), scales=y_plane[:, piece], in_=tile[:])
-        nc.sync.dma_start(out=out_words, in_=y_codes[:].bitcast(I32))
+            nc.sync.dma_start(out=out_words[:, cols], in_=y_codes[:, cols].bitcast(I32))
 
         for q in range(QUADS):
             queue = nc.scalar if q % 2 else nc.sync

@@ -207,7 +207,7 @@ def tile_picked_zuit_relu_po_kernel(
                         )
                     pair = bank[:, : 2 * CHUNK].rearrange("p (e j) -> p e j", e=2)
                     piece = slice(HALF * h + span.start, HALF * h + span.stop)
-                    nc.scalar.activation(out=y[:, rows, piece], in_=pair, func=ACT.Copy)
+                    nc.scalar.copy(out=y[:, rows, piece], in_=pair)
                 if u == 0:
                     nc.sync.dma_start(out=out_rows[:, rows, cols], in_=y[:, rows, cols])
                 elif h == 0:

@@ -153,7 +153,7 @@ def tile_picked_zuit_relu_po_kernel(
         out_rows = out_0.rearrange("(p t) j -> p t j", t=PACK)
         out_words = out_1[0].rearrange("p n t -> p (n t)").bitcast(I32)
         spans = [slice(lo, lo + CHUNK) for lo in range(0, HALF, CHUNK)]
-        row_pairs = [slice(0, 2), slice(2, 4)]
+        row_pairs = [[slice(0, 2), slice(2, 4)], [slice(1, 3), slice(0, 4, 3)]]
 
         hidden = [sbuf(f"hidden{h}", [P, PACK, HALF], BF16) for h in range(halves)]
         for t in range(PACK):
@@ -191,11 +191,10 @@ def tile_picked_zuit_relu_po_kernel(
         out_flat = out_0.rearrange("(p t) j -> p (t j)", t=PACK)
         for h in range(halves):
             cols = slice(HALF * h, HALF * (h + 1))
-            for u, rows in enumerate(row_pairs):
+            for u, rows in enumerate(row_pairs[h]):
                 for n, span in enumerate(spans):
                     bank = result_banks[4 * h + 2 * u + n]
-                    for e in range(2):
-                        t = 2 * u + e
+                    for e, t in enumerate(range(PACK)[rows]):
                         nc.tensor.matmul_mx(
                             out=bank[:, CHUNK * e : CHUNK * (e + 1)],
                             lhsT=w3_codes[:, 2 * P * t : 2 * P * (t + 1)].bitcast(FP4X4),
@@ -208,13 +207,13 @@ def tile_picked_zuit_relu_po_kernel(
                     pair = bank[:, : 2 * CHUNK].rearrange("p (e j) -> p e j", e=2)
                     piece = slice(HALF * h + span.start, HALF * h + span.stop)
                     nc.scalar.copy(out=y[:, rows, piece], in_=pair)
-                if u == 0:
+                if u == h:
                     nc.sync.dma_start(out=out_rows[:, rows, cols], in_=y[:, rows, cols])
                 elif h == 0:
-                    nc.sync.dma_start(out=out_rows[:, 2, cols], in_=y[:, 2, cols])
+                    nc.sync.dma_start(out=out_rows[:, 3, cols], in_=y[:, 3, cols])
                 else:
-                    tail = slice(2 * PAIRS + HALF, PACK * PAIRS)
-                    nc.sync.dma_start(out=out_flat[:, tail], in_=y_flat[:, tail])
+                    middle = slice(PAIRS + HALF, 3 * PAIRS)
+                    nc.sync.dma_start(out=out_flat[:, middle], in_=y_flat[:, middle])
 
         for h in range(halves):
             cols = slice(HALF * h, HALF * (h + 1))

@@ -39,7 +39,7 @@ def tile_picked_zuit_relu_po_kernel(
         psum = ctx.enter_context(tc.psum_pool(name="psum", bufs=1))
 
         def sbuf(name, shape, dtype, tag=None):
-            return keep.tile(shape, dtype, name=name, tag=tag or name, align_bytes=64)
+            return keep.tile(shape, dtype, name=name, tag=tag or name, align_bytes=256)
 
         offs_sb = keep.tile([P, PAIRS // 16], U16, name="offs_sb")
         item_sb = keep.tile([P, PAIRS // 16], U16, name="item_sb")

@@ -38,8 +38,8 @@ def tile_picked_zuit_relu_po_kernel(
         keep = ctx.enter_context(tc.tile_pool(name="keep", bufs=1))
         psum = ctx.enter_context(tc.psum_pool(name="psum", bufs=1))
 
-        def sbuf(name, shape, dtype, tag=None):
-            return keep.tile(shape, dtype, name=name, tag=tag or name, align_bytes=256)
+        def sbuf(name, shape, dtype, tag=None, align=256):
+            return keep.tile(shape, dtype, name=name, tag=tag or name, align_bytes=align)
 
         offs_sb = keep.tile([P, PAIRS // 16], U16, name="offs_sb")
         item_sb = keep.tile([P, PAIRS // 16], U16, name="item_sb")
@@ -48,8 +48,8 @@ def tile_picked_zuit_relu_po_kernel(
         w3s_raw = sbuf("w3s_raw", [P, WIDTH], U8)
         xs_table = sbuf("xs_table", [P, TABLE], U8)
         es_table = sbuf("es_table", [P, TABLE], U8)
-        w_raw = [sbuf(f"w_raw{g}", [P, PACK, WIDTH], F32) for g in range(passes)]
-        word_table = [sbuf(f"word_table{g}", [P, TABLE], I32) for g in range(passes)]
+        w_raw = [sbuf(f"w_raw{g}", [P, PACK * WIDTH], F32, align=4096) for g in range(passes)]
+        word_table = [sbuf(f"word_table{g}", [P, TABLE], I32, align=4096) for g in range(passes)]
 
         w_rows = [w1[K_PASS * g : K_PASS * (g + 1), :] for g in range(x_passes)] + [w2]
         word_rows = [x_words[g] for g in range(x_passes)] + [e_words[0]]
@@ -62,7 +62,7 @@ def tile_picked_zuit_relu_po_kernel(
         e_row = PACK * x_passes
 
         def load_weights(g):
-            nc.sync.dma_start(out=w_raw[g][:], in_=w_rows[g].rearrange("(p j) c -> p j c", j=PACK))
+            nc.sync.dma_start(out=w_raw[g][:], in_=w_rows[g].rearrange("(p j) c -> p (j c)", j=PACK))
 
         for q in range(QUADS):
             nc.gpsimd.dma_start(
@@ -96,7 +96,7 @@ def tile_picked_zuit_relu_po_kernel(
             grouped = sbuf(f"w_grouped{g}", [P, PACK * WIDTH], BF16)
             nc.scalar.activation(
                 out=grouped[:].rearrange("p (t m j) -> p m j t", t=PACK, j=PACK),
-                in_=w_raw[g][:].rearrange("p j (m t) -> p m j t", t=PACK),
+                in_=w_raw[g][:].rearrange("p (j m t) -> p m j t", j=PACK, t=PACK),
                 func=ACT.Copy,
             )
             w_codes[g] = sbuf(f"w_codes{g}", [P, WIDTH], U32)
@@ -186,7 +186,7 @@ def tile_picked_zuit_relu_po_kernel(
                 nc.vector.quantize_mx(out=h_codes[h][:, span].bitcast(FP8X4), scales=h_plane[h][:, span], in_=tile[:])
 
         result_banks = [banks[0][0], banks[0][1], banks[1][3], banks[0][2], banks[0][3]] + banks[1][:3]
-        y = sbuf("y", [P, PACK, PAIRS], F32)
+        y = sbuf("y", [P, PACK, PAIRS], F32, align=4096)
         y_flat = y[:].rearrange("p t j -> p (t j)")
         out_flat = out_0.rearrange("(p t) j -> p (t j)", t=PACK)
         for h in range(halves):

@@ -153,7 +153,7 @@ def tile_picked_zuit_relu_po_kernel(
         out_rows = out_0.rearrange("(p t) j -> p t j", t=PACK)
         out_words = out_1[0].rearrange("p n t -> p (n t)").bitcast(I32)
         spans = [slice(lo, lo + CHUNK) for lo in range(0, HALF, CHUNK)]
-        row_pairs = [[slice(0, 2), slice(2, 4)], [slice(1, 3), slice(0, 4, 3)]]
+        row_pairs = [slice(0, 2), slice(2, 4)]
 
         hidden = [sbuf(f"hidden{h}", [P, PACK, HALF], BF16) for h in range(halves)]
         for t in range(PACK):
@@ -187,11 +187,9 @@ def tile_picked_zuit_relu_po_kernel(
 
         result_banks = [banks[0][0], banks[0][1], banks[1][3], banks[0][2], banks[0][3]] + banks[1][:3]
         y = sbuf("y", [P, PACK, PAIRS], F32, align=4096)
-        y_flat = y[:].rearrange("p t j -> p (t j)")
-        out_flat = out_0.rearrange("(p t) j -> p (t j)", t=PACK)
         for h in range(halves):
             cols = slice(HALF * h, HALF * (h + 1))
-            for u, rows in enumerate(row_pairs[h]):
+            for u, rows in enumerate(row_pairs):
                 for n, span in enumerate(spans):
                     bank = result_banks[4 * h + 2 * u + n]
                     for e, t in enumerate(range(PACK)[rows]):
@@ -207,13 +205,7 @@ def tile_picked_zuit_relu_po_kernel(
                     pair = bank[:, : 2 * CHUNK].rearrange("p (e j) -> p e j", e=2)
                     piece = slice(HALF * h + span.start, HALF * h + span.stop)
                     nc.scalar.copy(out=y[:, rows, piece], in_=pair)
-                if u == h:
-                    nc.sync.dma_start(out=out_rows[:, rows, cols], in_=y[:, rows, cols])
-                elif h == 0:
-                    nc.sync.dma_start(out=out_rows[:, 3, cols], in_=y[:, 3, cols])
-                else:
-                    middle = slice(PAIRS + HALF, 3 * PAIRS)
-                    nc.sync.dma_start(out=out_flat[:, middle], in_=y_flat[:, middle])
+                nc.sync.dma_start(out=out_rows[:, rows, cols], in_=y[:, rows, cols])
 
         for h in range(halves):
             cols = slice(HALF * h, HALF * (h + 1))

@@ -22,7 +22,7 @@ WIDTH = 512
 HALF = 256
 CHUNK = 128
 QUADS = 4
-RUN = 4
+RUN = 2
 
 FLOPS = 2 * PAIRS * WIDTH * (1536 + 512 + 512)
 
@@ -155,7 +155,7 @@ def tile_picked_zuit_relu_po_kernel(
         spans = [slice(lo, lo + CHUNK) for lo in range(0, HALF, CHUNK)]
         row_pairs = [slice(0, 2), slice(2, 4)]
 
-        hidden = [sbuf(f"hidden{h}", [P, PACK, HALF], BF16) for h in range(halves)]
+        hidden = [sbuf(f"hidden{h}", [P, PACK, HALF], F32) for h in range(halves)]
         for t in range(PACK):
             if t % 2 == 0:
                 nc.scalar.activation(

@@ -72,7 +72,6 @@ def tile_picked_zuit_relu_po_kernel(
 
         load_weights(pass_order[0])
         nc.sync.dma_start(out=bias_sb[:], in_=bias.rearrange("(p t) o -> p (t o)", t=PACK))
-        nc.sync.dma_start(out=w3_raw[:].bitcast(I32), in_=w3_words[0].bitcast(I32))
         load_weights(pass_order[1])
         for q in range(QUADS):
             nc.sync.dma_start(
@@ -90,6 +89,7 @@ def tile_picked_zuit_relu_po_kernel(
             )
         for g in pass_order:
             nc.sync.dma_start(out=word_table[g][:], in_=word_rows[g].rearrange("p n t -> p (n t)").bitcast(I32))
+        nc.sync.dma_start(out=w3_raw[:].bitcast(I32), in_=w3_words[0].bitcast(I32))
 
         w_codes, w_scales = {}, {}
         for g in pass_order:
@@ -99,7 +99,8 @@ def tile_picked_zuit_relu_po_kernel(
                 in_=w_raw[g][:].rearrange("p (j m t) -> p m j t", j=PACK, t=PACK),
                 func=ACT.Copy,
             )
-            w_codes[g] = sbuf(f"w_codes{g}", [P, WIDTH], U32)
+            slot = f"word_table{pass_order[1]}" if g == pass_order[-1] else None
+            w_codes[g] = sbuf(f"w_codes{g}", [P, WIDTH], U32, tag=slot, align=4096)
             w_scales[g] = sbuf(f"w_scales{g}", [P, WIDTH], U8)
             nc.vector.quantize_mx(out=w_codes[g][:].bitcast(FP8X4), scales=w_scales[g][:], in_=grouped[:])
 
@@ -109,11 +110,11 @@ def tile_picked_zuit_relu_po_kernel(
         nc.vector.tensor_copy(es_picked[:], es_table[:].indirect(item_sb[:]))
         picked_scales = [xs_picked] * x_passes + [es_picked]
 
-        w3_codes = sbuf("w3_codes", [P, 2 * WIDTH], U8)
+        w3_early = sbuf("w3_early", [P, 2 * P * (PACK - 1)], U8)
         w3_plane = sbuf("w3_plane", [P, WIDTH], U8)
-        nc.vector.tensor_copy(
-            out=w3_codes[:].rearrange("p (t m b) -> p m t b", t=PACK, b=2),
-            in_=w3_raw[:].rearrange("p (m t b) -> p m t b", t=PACK, b=2),
+        nc.scalar.copy(
+            out=w3_early[:].bitcast(U16).rearrange("p (t m) -> p m t", t=PACK - 1),
+            in_=w3_raw[:].bitcast(U16).rearrange("p (m t) -> p m t", t=PACK)[:, :, : PACK - 1],
         )
         nc.vector.tensor_copy(
             out=w3_plane[:].rearrange("p (t m) -> p m t", t=PACK),
@@ -139,6 +140,13 @@ def tile_picked_zuit_relu_po_kernel(
                         start=(n == 0),
                         stop=(n == passes - 1),
                     )
+
+        w3_late = sbuf("w3_late", [P, 2 * P], U8, tag=f"word_table{pass_order[-1]}", align=4096)
+        nc.gpsimd.tensor_copy(
+            out=w3_late[:].rearrange("p (m b) -> p m b", b=2),
+            in_=w3_raw[:].rearrange("p (m t b) -> p m t b", t=PACK, b=2)[:, :, PACK - 1, :],
+        )
+        w3_codes = [w3_early[:, 2 * P * t : 2 * P * (t + 1)] for t in range(PACK - 1)] + [w3_late[:]]
 
         def weave(name, rows, tag=None):
             woven = sbuf(name, [P, PACK * CHUNK], BF16, tag=tag)
@@ -195,7 +203,7 @@ def tile_picked_zuit_relu_po_kernel(
                     for e, t in enumerate(range(PACK)[rows]):
                         nc.tensor.matmul_mx(
                             out=bank[:, CHUNK * e : CHUNK * (e + 1)],
-                            lhsT=w3_codes[:, 2 * P * t : 2 * P * (t + 1)].bitcast(FP4X4),
+                            lhsT=w3_codes[t].bitcast(FP4X4),
                             lhsT_scale=w3_plane[:, P * t : P * (t + 1)],
                             rhs=h_codes[h][:, span].bitcast(FP8X4),
                             rhs_scale=h_plane[h][:, span],

@@ -71,6 +71,8 @@ def tile_picked_zuit_relu_po_kernel(
             )
 
         load_weights(pass_order[0])
+        nc.sync.dma_start(offs_sb[:], offs)
+        nc.sync.dma_start(item_sb[:], item)
         nc.sync.dma_start(out=bias_sb[:], in_=bias.rearrange("(p t) o -> p (t o)", t=PACK))
         load_weights(pass_order[1])
         for q in range(QUADS):
@@ -79,14 +81,12 @@ def tile_picked_zuit_relu_po_kernel(
                 in_=e_scales[0, 4 * q : 4 * q + 4, :].bitcast(I32),
             )
         load_weights(pass_order[2])
-        nc.sync.dma_start(offs_sb[:], offs)
-        nc.sync.dma_start(item_sb[:], item)
-        load_weights(pass_order[3])
         for q in range(QUADS):
             nc.sync.dma_start(
                 out=w3s_raw[32 * q : 32 * q + 4, :].bitcast(I32),
                 in_=w3_scales[0, 4 * q : 4 * q + 4, :].bitcast(I32),
             )
+        load_weights(pass_order[3])
         for g in pass_order:
             nc.sync.dma_start(out=word_table[g][:], in_=word_rows[g].rearrange("p n t -> p (n t)").bitcast(I32))
         nc.sync.dma_start(out=w3_raw[:].bitcast(I32), in_=w3_words[0].bitcast(I32))
@@ -104,7 +104,7 @@ def tile_picked_zuit_relu_po_kernel(
             w_scales[g] = sbuf(f"w_scales{g}", [P, WIDTH], U8)
             nc.vector.quantize_mx(out=w_codes[g][:].bitcast(FP8X4), scales=w_scales[g][:], in_=grouped[:])
 
-        xs_picked = sbuf("xs_picked", [P, PAIRS], U8)
+        xs_picked = sbuf("xs_picked", [P, PAIRS], U8, tag=f"w_grouped{pass_order[1]}")
         es_picked = sbuf("es_picked", [P, PAIRS], U8)
         nc.vector.tensor_copy(xs_picked[:], xs_table[:].indirect(offs_sb[:]))
         nc.vector.tensor_copy(es_picked[:], es_table[:].indirect(item_sb[:]))

@@ -75,16 +75,16 @@ def tile_picked_zuit_relu_po_kernel(
         nc.sync.dma_start(item_sb[:], item)
         nc.sync.dma_start(out=bias_sb[:], in_=bias.rearrange("(p t) o -> p (t o)", t=PACK))
         load_weights(pass_order[1])
-        for q in range(QUADS):
+        for r in range(PACK):
             nc.sync.dma_start(
-                out=es_table[32 * q + e_row : 32 * q + e_row + 4, :].bitcast(I32),
-                in_=e_scales[0, 4 * q : 4 * q + 4, :].bitcast(I32),
+                out=es_table[e_row + r : P : 32, :].bitcast(I32),
+                in_=e_scales[0, r : 16 : 4, :].bitcast(I32),
             )
         load_weights(pass_order[2])
-        for q in range(QUADS):
+        for r in range(PACK):
             nc.sync.dma_start(
-                out=w3s_raw[32 * q : 32 * q + 4, :].bitcast(I32),
-                in_=w3_scales[0, 4 * q : 4 * q + 4, :].bitcast(I32),
+                out=w3s_raw[r:P:32, :].bitcast(I32),
+                in_=w3_scales[0, r:16:4, :].bitcast(I32),
             )
         load_weights(pass_order[3])
         for g in pass_order:
@@ -223,8 +223,6 @@ def tile_picked_zuit_relu_po_kernel(
                 nc.vector.quantize_mx(out=y_codes[:, piece].bitcast(FP8X4), scales=y_plane[:, piece], in_=tile[:])
             nc.sync.dma_start(out=out_words[:, cols], in_=y_codes[:, cols].bitcast(I32))
 
-        for q in range(QUADS):
-            queue = nc.scalar if q % 2 else nc.sync
-            queue.dma_start(
-                out=out_2[0, 4 * q : 4 * q + 4, :].bitcast(I32), in_=y_plane[32 * q : 32 * q + 4, :].bitcast(I32)
-            )
+        for r in range(PACK):
+            queue = nc.scalar if r % 2 else nc.sync
+            queue.dma_start(out=out_2[0, r:16:4, :].bitcast(I32), in_=y_plane[r:P:32, :].bitcast(I32))

from contextlib import ExitStack

import concourse.mybir as mybir

F32 = mybir.dt.float32
BF16 = mybir.dt.bfloat16
I32 = mybir.dt.int32
U32 = mybir.dt.uint32
U16 = mybir.dt.uint16
U8 = mybir.dt.uint8
FP8X4 = mybir.dt.float8_e4m3fn_x4
FP4X4 = mybir.dt.float4_e2m1fn_x4
ACT = mybir.ActivationFunctionType
ALU = mybir.AluOpType

P = 128
PACK = 4
K_PASS = P * PACK
TABLE = 2048
PAIRS = 512
WIDTH = 512
HALF = 256
CHUNK = 128
QUADS = 4
RUN = 2

FLOPS = 2 * PAIRS * WIDTH * (1536 + 512 + 512)


def tile_picked_zuit_relu_po_kernel(
    tc, x_words, x_scales, e_words, e_scales, w1, w2, w3_words, w3_scales, bias, offs, item, out_0, out_1, out_2
):
    nc = tc.nc
    x_passes = x_words.shape[0]
    passes = x_passes + 1

    with ExitStack() as ctx:
        keep = ctx.enter_context(tc.tile_pool(name="keep", bufs=1))
        psum = ctx.enter_context(tc.psum_pool(name="psum", bufs=1))

        def sbuf(name, shape, dtype, tag=None, align=256):
            return keep.tile(shape, dtype, name=name, tag=tag or name, align_bytes=align)

        offs_sb = keep.tile([P, PAIRS // 16], U16, name="offs_sb")
        item_sb = keep.tile([P, PAIRS // 16], U16, name="item_sb")
        bias_sb = sbuf("bias_sb", [P, PACK], F32)
        w3_raw = sbuf("w3_raw", [P, 2 * WIDTH], U8)
        w3s_raw = sbuf("w3s_raw", [P, WIDTH], U8)
        xs_table = sbuf("xs_table", [P, TABLE], U8)
        es_table = sbuf("es_table", [P, TABLE], U8)
        w_raw = [sbuf(f"w_raw{g}", [P, PACK * WIDTH], F32, align=4096) for g in range(passes)]
        word_table = [sbuf(f"word_table{g}", [P, TABLE], I32, align=4096) for g in range(passes)]

        w_rows = [w1[K_PASS * g : K_PASS * (g + 1), :] for g in range(x_passes)] + [w2]
        word_rows = [x_words[g] for g in range(x_passes)] + [e_words[0]]
        lists = [offs_sb] * x_passes + [item_sb]
        pass_order = [0, 1, 3, 2]

        nc.gpsimd.memset(xs_table[:].bitcast(I32), 0)
        nc.vector.memset(es_table[:].bitcast(I32), 0)
        nc.vector.memset(w3s_raw[:].bitcast(I32), 0)
        e_row = PACK * x_passes

        def load_weights(g):
            nc.sync.dma_start(out=w_raw[g][:], in_=w_rows[g].rearrange("(p j) c -> p (j c)", j=PACK))

        for q in range(QUADS):
            nc.gpsimd.dma_start(
                out=xs_table[32 * q : 32 * q + PACK * x_passes, :].bitcast(I32),
                in_=x_scales[:, 4 * q : 4 * q + 4, :].bitcast(I32),
            )

        load_weights(pass_order[0])
        nc.sync.dma_start(offs_sb[:], offs)
        nc.sync.dma_start(item_sb[:], item)
        nc.sync.dma_start(out=bias_sb[:], in_=bias.rearrange("(p t) o -> p (t o)", t=PACK))
        load_weights(pass_order[1])
        for r in range(PACK):
            nc.sync.dma_start(
                out=es_table[e_row + r : P : 32, :].bitcast(I32),
                in_=e_scales[0, r : 16 : 4, :].bitcast(I32),
            )
        load_weights(pass_order[2])
        for r in range(PACK):
            nc.sync.dma_start(
                out=w3s_raw[r:P:32, :].bitcast(I32),
                in_=w3_scales[0, r:16:4, :].bitcast(I32),
            )
        load_weights(pass_order[3])
        for g in pass_order:
            nc.sync.dma_start(out=word_table[g][:], in_=word_rows[g].rearrange("p n t -> p (n t)").bitcast(I32))
        nc.sync.dma_start(out=w3_raw[:].bitcast(I32), in_=w3_words[0].bitcast(I32))

        w_codes, w_scales = {}, {}
        for g in pass_order:
            grouped = sbuf(f"w_grouped{g}", [P, PACK * WIDTH], BF16)
            nc.scalar.activation(
                out=grouped[:].rearrange("p (t m j) -> p m j t", t=PACK, j=PACK),
                in_=w_raw[g][:].rearrange("p (j m t) -> p m j t", j=PACK, t=PACK),
                func=ACT.Copy,
            )
            slot = f"word_table{pass_order[1]}" if g == pass_order[-1] else None
            w_codes[g] = sbuf(f"w_codes{g}", [P, WIDTH], U32, tag=slot, align=4096)
            w_scales[g] = sbuf(f"w_scales{g}", [P, WIDTH], U8)
            nc.vector.quantize_mx(out=w_codes[g][:].bitcast(FP8X4), scales=w_scales[g][:], in_=grouped[:])

        xs_picked = sbuf("xs_picked", [P, PAIRS], U8, tag=f"w_grouped{pass_order[1]}")
        es_picked = sbuf("es_picked", [P, PAIRS], U8)
        nc.vector.tensor_copy(xs_picked[:], xs_table[:].indirect(offs_sb[:]))
        nc.vector.tensor_copy(es_picked[:], es_table[:].indirect(item_sb[:]))
        picked_scales = [xs_picked] * x_passes + [es_picked]

        w3_early = sbuf("w3_early", [P, 2 * P * (PACK - 1)], U8)
        w3_plane = sbuf("w3_plane", [P, WIDTH], U8)
        nc.scalar.copy(
            out=w3_early[:].bitcast(U16).rearrange("p (t m) -> p m t", t=PACK - 1),
            in_=w3_raw[:].bitcast(U16).rearrange("p (m t) -> p m t", t=PACK)[:, :, : PACK - 1],
        )
        nc.vector.tensor_copy(
            out=w3_plane[:].rearrange("p (t m) -> p m t", t=PACK),
            in_=w3s_raw[:].rearrange("p (m t) -> p m t", t=PACK),
        )

        halves = PAIRS // HALF
        banks = [[psum.tile([P, 512], F32, name=f"bank{h}_{t}") for t in range(PACK)] for h in range(halves)]

        for n, g in enumerate(pass_order):
            for h in range(halves):
                picked = sbuf(f"picked{g}_{h}", [P, HALF], U32)
                entries = lists[g][:, h * HALF // 16 : (h + 1) * HALF // 16]
                nc.vector.tensor_copy(picked[:], word_table[g][:].bitcast(U32).indirect(entries))
                for t in range(PACK):
                    cols = slice(P * t, P * (t + 1))
                    nc.tensor.matmul_mx(
                        out=banks[h][t][:, :HALF],
                        lhsT=w_codes[g][:, cols].bitcast(FP8X4),
                        lhsT_scale=w_scales[g][:, cols],
                        rhs=picked[:].bitcast(FP8X4),
                        rhs_scale=picked_scales[g][PACK * g :, h * HALF : (h + 1) * HALF],
                        start=(n == 0),
                        stop=(n == passes - 1),
                    )

        w3_late = sbuf("w3_late", [P, 2 * P], U8, tag=f"word_table{pass_order[-1]}", align=4096)
        nc.gpsimd.tensor_copy(
            out=w3_late[:].rearrange("p (m b) -> p m b", b=2),
            in_=w3_raw[:].rearrange("p (m t b) -> p m t b", t=PACK, b=2)[:, :, PACK - 1, :],
        )
        w3_codes = [w3_early[:, 2 * P * t : 2 * P * (t + 1)] for t in range(PACK - 1)] + [w3_late[:]]

        def weave(name, rows, tag=None):
            woven = sbuf(name, [P, PACK * CHUNK], BF16, tag=tag)
            nc.vector.tensor_copy(
                out=woven[:].rearrange("p (c i t) -> p c t i", i=RUN, t=PACK),
                in_=rows.rearrange("p t (c i) -> p c t i", i=RUN),
            )
            return woven

        y_codes = sbuf("y_codes", [P, PAIRS], U32)
        y_plane = sbuf("y_plane", [P, PAIRS], U8)
        out_rows = out_0.rearrange("(p t) j -> p t j", t=PACK)
        out_words = out_1[0].rearrange("p n t -> p (n t)").bitcast(I32)
        spans = [slice(lo, lo + CHUNK) for lo in range(0, HALF, CHUNK)]
        row_pairs = [slice(0, 2), slice(2, 4)]

        hidden = [sbuf(f"hidden{h}", [P, PACK, HALF], F32) for h in range(halves)]
        for t in range(PACK):
            if t % 2 == 0:
                nc.scalar.activation(
                    out=hidden[0][:, t, :], in_=banks[0][t][:, :HALF], func=ACT.Relu, bias=bias_sb[:, t : t + 1]
                )
                continue
            for span in spans if t == PACK - 1 else [slice(0, HALF)]:
                nc.vector.tensor_scalar(
                    out=hidden[0][:, t, span],
                    in0=banks[0][t][:, span],
                    scalar1=bias_sb[:, t : t + 1],
                    scalar2=0.0,
                    op0=ALU.add,
                    op1=ALU.max,
                )
        pieces = [(t, slice(0, HALF)) for t in range(2)] + [(t, span) for span in spans for t in range(2, PACK)]
        for t, span in pieces:
            nc.scalar.activation(
                out=hidden[1][:, t, span], in_=banks[1][t][:, span], func=ACT.Relu, bias=bias_sb[:, t : t + 1]
            )

        h_codes, h_plane = [], []
        for h in range(halves):
            woven = [weave(f"h_woven{h}_{n}", hidden[h][:, :, span]) for n, span in enumerate(spans)]
            h_codes.append(sbuf(f"h_codes{h}", [P, HALF], U32))
            h_plane.append(sbuf(f"h_plane{h}", [P, HALF], U8))
            for span, tile in zip(spans, woven):
                nc.vector.quantize_mx(out=h_codes[h][:, span].bitcast(FP8X4), scales=h_plane[h][:, span], in_=tile[:])

        result_banks = [banks[0][0], banks[0][1], banks[1][3], banks[0][2], banks[0][3]] + banks[1][:3]
        y = sbuf("y", [P, PACK, PAIRS], F32, align=4096)
        for h in range(halves):
            cols = slice(HALF * h, HALF * (h + 1))
            for u, rows in enumerate(row_pairs):
                for n, span in enumerate(spans):
                    bank = result_banks[4 * h + 2 * u + n]
                    for e, t in enumerate(range(PACK)[rows]):
                        nc.tensor.matmul_mx(
                            out=bank[:, CHUNK * e : CHUNK * (e + 1)],
                            lhsT=w3_codes[t].bitcast(FP4X4),
                            lhsT_scale=w3_plane[:, P * t : P * (t + 1)],
                            rhs=h_codes[h][:, span].bitcast(FP8X4),
                            rhs_scale=h_plane[h][:, span],
                            start=True,
                            stop=True,
                        )
                    pair = bank[:, : 2 * CHUNK].rearrange("p (e j) -> p e j", e=2)
                    piece = slice(HALF * h + span.start, HALF * h + span.stop)
                    nc.scalar.copy(out=y[:, rows, piece], in_=pair)
                nc.sync.dma_start(out=out_rows[:, rows, cols], in_=y[:, rows, cols])

        for h in range(halves):
            cols = slice(HALF * h, HALF * (h + 1))
            woven = [weave(f"y_woven{h}_{n}", y[:, :, HALF * h + span.start : HALF * h + span.stop], f"h_woven{1 - h}_{1 - n}") for n, span in enumerate(spans)]
            for n, tile in enumerate(woven):
                piece = slice(HALF * h + CHUNK * n, HALF * h + CHUNK * (n + 1))
                nc.vector.quantize_mx(out=y_codes[:, piece].bitcast(FP8X4), scales=y_plane[:, piece], in_=tile[:])
            nc.sync.dma_start(out=out_words[:, cols], in_=y_codes[:, cols].bitcast(I32))

        for r in range(PACK):
            queue = nc.scalar if r % 2 else nc.sync
            queue.dma_start(out=out_2[0, r:16:4, :].bitcast(I32), in_=y_plane[r:P:32, :].bitcast(I32))
